import numpy as np
import ml_dtypes


def mxq(x, axis, fmt="e4m3"):
    dtype, down = {"e4m3": (ml_dtypes.float8_e4m3fn, 7), "e5m2": (ml_dtypes.float8_e5m2, 14)}[fmt]
    v = np.moveaxis(np.asarray(x, np.float32).astype(ml_dtypes.bfloat16).astype(np.float64), axis, -1)
    blocks = v.reshape(v.shape[:-1] + (-1, 32))
    amax = np.abs(blocks).max(-1, keepdims=True)
    byte = np.maximum(np.where(amax > 0, np.frexp(amax)[1] - 1 + 127, 0) - down, 1)
    scale = np.exp2(byte - 127.0)
    codes = (blocks / scale).astype(np.float32).astype(dtype).astype(np.float64)
    return np.moveaxis((codes * scale).reshape(v.shape), -1, axis)


WIDE = False


def mx_kscale(k):
    if not WIDE:
        return np.ones(k)
    levels = np.array([24, -24, 12, -12, 0])
    if k % 512:
        return np.exp2(np.random.permutation(np.resize(levels, k // 32))).repeat(32)
    a = np.empty((k // 512, 16))
    for p in range(k // 512):
        a[p, :8] = np.random.permutation(np.resize(levels, 8))
        for g in range(8):
            far = levels[np.abs(levels - a[p, g]) >= 10]
            a[p, g + 8] = far[np.random.randint(len(far))]
    return np.exp2(a.ravel()).repeat(32)


def f64(x):
    return np.asarray(x).astype(np.float64)


def striped8(idx):
    return np.concatenate([v.reshape(-1, 16).T for v in idx]).astype(np.uint16)


def unstriped8(offs):
    return np.stack([offs[16 * g:16 * g + 16].T.reshape(-1) for g in range(8)]).astype(np.int64)


E2M1 = np.array([0.0, 0.5, 1.0, 1.5, 2.0, 3.0, 4.0, 6.0, -0.0, -0.5, -1.0, -1.5, -2.0, -3.0, -4.0, -6.0])


def pack_weight(w, fmt):
    k, n = w.shape
    w = f64(np.asarray(w, np.float32).astype(ml_dtypes.bfloat16)).reshape(k // 32, 32, n)
    amax = np.abs(w).max(1)
    if fmt == "e4m3":
        byte = np.frexp(amax)[1] - 1 + 127 - 7
    else:
        mant, ex = np.frexp(amax / 6.0)
        byte = np.where(mant > 0.5, ex, ex - 1) + 127
    byte = np.clip(np.where(amax > 0, byte, 1), 1, 254)
    scaled = (w * np.exp2(127.0 - byte)[:, None, :]).reshape(k, n).astype(np.float32)
    by_word = np.ascontiguousarray(scaled.reshape(k // 512, 128, 4, n).transpose(0, 1, 3, 2))
    if fmt == "e4m3":
        words = by_word.astype(ml_dtypes.float8_e4m3fn).view(np.uint8)
    else:
        c = by_word.astype(ml_dtypes.float4_e2m1fn).view(np.uint8) & 0xF
        words = (c[..., 0::2] | (c[..., 1::2] << 4)).reshape(k // 512, 128, 2 * n)
    return np.ascontiguousarray(words), np.ascontiguousarray(byte.astype(np.uint8).reshape(k // 512, 16, n))


def unpack_weight(words, scales, fmt):
    g, _, n = scales.shape
    words = np.ascontiguousarray(words).reshape(g, 128, n, -1)
    if fmt == "e4m3":
        vals = words.view(ml_dtypes.float8_e4m3fn).astype(np.float64)
    else:
        nib = np.empty((g, 128, n, 4), np.uint8)
        nib[..., 0::2] = words & 0xF
        nib[..., 1::2] = words >> 4
        vals = E2M1[nib]
    vals = vals * np.repeat(np.exp2(scales.astype(np.float64) - 127.0), 8, axis=1)[..., None]
    return vals.transpose(0, 1, 3, 2).reshape(g * 512, n)


def silu(f):
    return f / (1.0 + np.exp(-np.maximum(f, -700.0)))


K, R, N, T, J = 512, 512, 512, 2048, 1024


def setup_inputs():
    n = np.random.standard_normal
    s = mx_kscale(K)[:, None]
    u = mx_kscale(R)[:, None]
    p_wg = pack_weight(n((K, R)) / np.sqrt(K) / s, "e4m3")
    p_wd = pack_weight(n((R, N)) / np.sqrt(R) / u, "e4m3")
    return {
        "xT": (n((K, T)) * s).astype(np.float32),
        "wgt": np.repeat(np.random.uniform(0.5, 2.0, (8, J)), 16, axis=0).astype(np.float32),
        "wg_words": p_wg[0],
        "wg_scales": p_wg[1],
        "wu": (n((K, R)) / np.sqrt(K) / s * u.T).astype(np.float32),
        "wd_words": p_wd[0],
        "wd_scales": p_wd[1],
        "b": (0.3 * n(N)).astype(np.float32),
        "offs": striped8(np.stack([np.random.permutation(T)[:J] for _ in range(8)])),
    }


def reference(xT, wgt, wg_words, wg_scales, wu, wd_words, wd_scales, b, offs):
    idx = unstriped8(offs)
    rows = np.arange(K)
    xg = f64(wgt)[rows // 4 % 128] * f64(xT)[rows[:, None], idx[rows % 512 // 64]]
    xT_ = mxq(xg, 0, "e4m3")
    wg_ = unpack_weight(wg_words, wg_scales, "e4m3")
    wu_ = mxq(f64(wu), 0, "e4m3")
    ga = wg_.T @ xT_
    ub = wu_.T @ xT_
    h = silu(ga) * ub
    h_ = mxq(h, 0, "e4m3")
    wd_ = unpack_weight(wd_words, wd_scales, "e4m3")
    y = wd_.T @ h_
    return y + f64(b)[:, None]

@@ -1,0 +1,221 @@
+from contextlib import ExitStack
+
+import concourse.mybir as mybir
+
+K, R, N, T, J = 512, 512, 512, 2048, 1024
+FLOPS = 2 * J * (2 * K * R + R * N)
+
+F32 = mybir.dt.float32
+BF16 = mybir.dt.bfloat16
+I32 = mybir.dt.int32
+U16 = mybir.dt.uint16
+U8 = mybir.dt.uint8
+FP8X4 = mybir.dt.float8_e4m3fn_x4
+MULT = mybir.AluOpType.mult
+ACT = mybir.ActivationFunctionType
+
+P = 128
+PACK = 4
+CHUNK = 128
+CHUNKS = J // CHUNK
+HALF = J // 2
+PER_COLUMN = 16
+
+
+def tile_list_silu_bias_kernel(
+    tc, xT, wgt, wg_words, wg_scales, wu, wd_words, wd_scales, b, offs, out
+):
+    nc = tc.nc
+    with ExitStack() as ctx:
+        keep = ctx.enter_context(tc.tile_pool(name="keep", bufs=1))
+        psum = ctx.enter_context(tc.psum_pool(name="psum", bufs=1))
+
+        offsets = keep.tile([P, J // PER_COLUMN], U16, name="offsets")
+        planes = [keep.tile([P, T], F32, name="plane%d" % i) for i in range(PACK)]
+        wgt_sb = keep.tile([P, J], F32, name="wgt_sb")
+        wg_raw = keep.tile([P, R], I32, name="wg_raw", align_bytes=64)
+        wg_raw_scales = keep.tile([P, R], U8, name="wg_raw_scales", align_bytes=64)
+        wg_codes = keep.tile([P, R], I32, name="wg_codes", align_bytes=64)
+        wg_plane = keep.tile([P, R], U8, name="wg_plane", align_bytes=64)
+        wu_raw = [keep.tile([P, PACK, R // 2], F32, name="wu_raw%d" % h) for h in range(2)]
+        wu_bf = keep.tile([P, PACK, P, PACK], BF16, name="wu_bf", align_bytes=64)
+        wu_codes = keep.tile([P, R], I32, name="wu_codes", align_bytes=64)
+        wu_plane = keep.tile([P, R], U8, name="wu_plane", align_bytes=64)
+        wd_codes = keep.tile([P, N], I32, name="wd_codes", align_bytes=64)
+        wd_plane = keep.tile([P, N], U8, name="wd_plane", align_bytes=64)
+        bias = keep.tile([P, N // P], F32, name="bias")
+        zero = keep.tile([P, 1], F32, name="zero")
+        no_bias = keep.tile([P, 1], F32, name="no_bias")
+        picked = keep.tile([P, PACK, J], F32, name="picked")
+        xg_bf = keep.tile([P, J, PACK], BF16, name="xg_bf", align_bytes=64)
+        xg_codes = keep.tile([P, J], I32, name="xg_codes", align_bytes=64)
+        xg_plane = keep.tile([P, J], U8, name="xg_plane", align_bytes=64)
+        gate = keep.tile([P, J, PACK], F32, name="gate")
+        h_bf = keep.tile([P, J, PACK], BF16, name="h_bf", align_bytes=64)
+        h_codes = keep.tile([P, J], I32, name="h_codes", align_bytes=64)
+        h_plane = keep.tile([P, J], U8, name="h_plane", align_bytes=64)
+        result = keep.tile([P, N // P, J], F32, name="result")
+
+        x_planes = xT.rearrange("(p i) t -> i p t", i=PACK)
+        wu_rows = wu.rearrange("(p i) r -> p i r", i=PACK)
+        out_rows = out.rearrange("(u p) j -> p u j", p=P)
+
+        def words(dram):
+            return dram[0].rearrange("p n i -> p (n i)").bitcast(I32)
+
+        def load_scale_rows(queue, plane, dram):
+            for q in range(4):
+                queue.dma_start(
+                    out=plane[32 * q : 32 * q + 4, :].bitcast(I32),
+                    in_=dram[0, 4 * q : 4 * q + 4, :].bitcast(I32),
+                )
+
+        nc.vector.memset(wg_raw_scales[:].bitcast(I32), 0)
+        nc.gpsimd.memset(wd_plane[:].bitcast(I32), 0)
+        nc.vector.memset(zero[:], 0.0)
+
+        nc.sync.dma_start(offsets[:], offs)
+        nc.sync.dma_start(out=wg_raw[:], in_=words(wg_words))
+        nc.sync.dma_start(out=wgt_sb[:, :HALF], in_=wgt[:, :HALF])
+        nc.sync.dma_start(out=planes[0][:], in_=x_planes[0])
+        load_scale_rows(nc.scalar, wg_raw_scales, wg_scales)
+        nc.scalar.activation(no_bias[:], zero[:], ACT.Silu)
+        nc.sync.dma_start(out=wgt_sb[:, HALF:], in_=wgt[:, HALF:])
+        for i in range(1, PACK):
+            nc.sync.dma_start(out=planes[i][:], in_=x_planes[i])
+        for h in range(2):
+            nc.sync.dma_start(out=wu_raw[h][:], in_=wu_rows[:, :, h * (R // 2) : (h + 1) * (R // 2)])
+        nc.sync.dma_start(out=wd_codes[:], in_=words(wd_words))
+        load_scale_rows(nc.sync, wd_plane, wd_scales)
+        with nc.allow_non_contiguous_dma(reason="one bias value a partition"):
+            nc.sync.dma_start(out=bias[:], in_=b.rearrange("(u p) -> p u", p=P))
+
+        nc.vector.tensor_copy(
+            out=wg_codes[:].rearrange("p (t m) -> p m t", t=PACK),
+            in_=wg_raw[:].rearrange("p (m t) -> p m t", t=PACK),
+        )
+        nc.vector.tensor_copy(
+            out=wg_plane[:].rearrange("p (t m) -> p m t", t=PACK),
+            in_=wg_raw_scales[:].rearrange("p (m t) -> p m t", t=PACK),
+        )
+
+        def gather(i, first, last):
+            nc.vector.tensor_tensor(
+                picked[:, i, first:last],
+                planes[i][:].indirect(offsets[:, first // PER_COLUMN : last // PER_COLUMN]),
+                wgt_sb[:, first:last],
+                MULT,
+            )
+
+        def copy_on(engine, dst, src):
+            if engine == "scalar":
+                nc.scalar.copy(out=dst, in_=src)
+            else:
+                nc.vector.tensor_copy(out=dst, in_=src)
+
+        def round_pair(engine, i, first, last):
+            copy_on(
+                engine,
+                xg_bf[:, first:last, i : i + 2],
+                picked[:, i : i + 2, first:last].rearrange("p i j -> p j i"),
+            )
+
+        def quantize(codes, plane, src, first, last):
+            nc.vector.quantize_mx(
+                out=codes[:, first:last].bitcast(FP8X4),
+                scales=plane[:, first:last],
+                in_=src[:, first:last, :].rearrange("p j i -> p (j i)"),
+            )
+
+        def product(dst, w_codes, w_plane, tile, a_codes, a_plane, first, last):
+            cols = slice(tile * P, (tile + 1) * P)
+            nc.tensor.matmul_mx(
+                out=dst,
+                lhsT=w_codes[:, cols].bitcast(FP8X4),
+                lhsT_scale=w_plane[:, cols],
+                rhs=a_codes[:, first:last].bitcast(FP8X4),
+                rhs_scale=a_plane[:, first:last],
+                start=True,
+                stop=True,
+            )
+
+        def round_wu(engine, h):
+            copy_on(
+                engine,
+                wu_bf[:, :, 64 * h : 64 * (h + 1), :].rearrange("p t m i -> p m i t"),
+                wu_raw[h][:].rearrange("p i (m t) -> p m i t", t=PACK),
+            )
+
+        def gate_chunk(c):
+            first, last = c * CHUNK, (c + 1) * CHUNK
+            quantize(xg_codes, xg_plane, xg_bf, first, last)
+            ga = psum.tile([P, PACK, CHUNK], F32, name="ga", bufs=2)
+            for t in range(PACK):
+                product(ga[:, t, :], wg_codes, wg_plane, t, xg_codes, xg_plane, first, last)
+            nc.scalar.activation(
+                gate[:, first:last, :], ga[:].rearrange("p t j -> p j t"), ACT.Silu, bias=no_bias[:]
+            )
+
+        def up_chunk(c):
+            first, last = c * CHUNK, (c + 1) * CHUNK
+            ub = psum.tile([P, PACK, CHUNK], F32, name="ub", bufs=2)
+            for t in range(PACK):
+                product(ub[:, t, :], wu_codes, wu_plane, t, xg_codes, xg_plane, first, last)
+            nc.vector.tensor_tensor(
+                h_bf[:, first:last, :], ub[:].rearrange("p t j -> p j t"), gate[:, first:last, :], MULT
+            )
+
+        def down(first, last, engines):
+            for pair in range(2):
+                y = psum.tile([P, 2, last - first], F32, name="y", bufs=4)
+                for s in range(2):
+                    product(y[:, s, :], wd_codes, wd_plane, 2 * pair + s, h_codes, h_plane, first, last)
+                for s in range(2):
+                    u = 2 * pair + s
+                    if engines[pair] == "scalar":
+                        nc.scalar.activation(
+                            result[:, u, first:last], y[:, s, :], ACT.Identity, bias=bias[:, u : u + 1]
+                        )
+                    else:
+                        nc.vector.tensor_scalar_add(result[:, u, first:last], y[:, s, :], bias[:, u : u + 1])
+                nc.sync.dma_start(
+                    out=out_rows[:, 2 * pair : 2 * pair + 2, first:last],
+                    in_=result[:, 2 * pair : 2 * pair + 2, first:last],
+                )
+
+        for i in range(PACK - 1):
+            for first in (0, HALF):
+                gather(i, first, first + HALF)
+                if i == 1:
+                    round_pair("scalar", 0, first, first + HALF)
+
+        for step in range(CHUNKS + 2):
+            if step < CHUNKS:
+                gather(PACK - 1, step * CHUNK, (step + 1) * CHUNK)
+            if 1 <= step <= CHUNKS:
+                c = step - 1
+                round_pair("scalar" if c < 4 else "vector", 2, c * CHUNK, (c + 1) * CHUNK)
+            if step == 4:
+                round_wu("scalar", 0)
+            if step == 7:
+                round_wu("vector", 1)
+            if step == 8:
+                nc.vector.quantize_mx(
+                    out=wu_codes[:].bitcast(FP8X4),
+                    scales=wu_plane[:],
+                    in_=wu_bf[:].rearrange("p t m i -> p (t m i)"),
+                )
+            if step >= 2:
+                gate_chunk(step - 2)
+
+        spans = {1: (0, 256, ("scalar", "scalar")), 3: (256, 512, ("scalar", "scalar")),
+                 5: (512, 768, ("scalar", "scalar")), 6: (768, 896, ("scalar", "scalar")),
+                 7: (896, 1024, ("scalar", "vector"))}
+        for step in range(CHUNKS + 1):
+            if step < CHUNKS:
+                up_chunk(step)
+            if step >= 1:
+                c = step - 1
+                quantize(h_codes, h_plane, h_bf, c * CHUNK, (c + 1) * CHUNK)
+                if c in spans:
+                    down(*spans[c])

@@ -20,6 +20,20 @@ CHUNK = 128
 CHUNKS = J // CHUNK
 HALF = J // 2
 PER_COLUMN = 16
+LOADS = ["wgt0","x0","wgt1","x1","wg","wgs","x2","x3","wu0","wu1","wd"]
+PICK_SPANS = [[1,"vector"],[1,"vector"],[1,"scalar"],[1,"scalar"],[1,"vector"],[1,"scalar"],[1,"scalar"],[1,"scalar"]]
+WU_ENGINES = ["scalar","vector"]
+WU_STEPS = [-1,3,3]
+UP_LAG = 4
+DOWN_SPANS = [[2,"scalar","scalar"],[2,"scalar","scalar"],[1,"vector","scalar"],[1,"scalar","scalar"],[1,"scalar","vector"],[1,"vector","scalar"]]
+WGT_SPLIT = 512
+EARLY = (512, 512)
+BUFS = (2, 2, 4)
+STAGE_ORDER = (0, 1, 2, 3, 4, 5, 6)
+GATE_LAG = 2
+DOWN_LAG = 1
+STORE_ENDS = [2,4,5,6,7,8]
+STORES = {}
 
 
 def tile_list_silu_bias_kernel(
@@ -37,7 +51,7 @@ def tile_list_silu_bias_kernel(
         wg_raw_scales = keep.tile([P, R], U8, name="wg_raw_scales", align_bytes=64)
         wg_codes = keep.tile([P, R], I32, name="wg_codes", align_bytes=64)
         wg_plane = keep.tile([P, R], U8, name="wg_plane", align_bytes=64)
-        wu_raw = [keep.tile([P, PACK, R // 2], F32, name="wu_raw%d" % h) for h in range(2)]
+        wu_raw = keep.tile([P, PACK, R], F32, name="wu_raw")
         wu_bf = keep.tile([P, PACK, P, PACK], BF16, name="wu_bf", align_bytes=64)
         wu_codes = keep.tile([P, R], I32, name="wu_codes", align_bytes=64)
         wu_plane = keep.tile([P, R], U8, name="wu_plane", align_bytes=64)
@@ -71,21 +85,32 @@ def tile_list_silu_bias_kernel(
                 )
 
         nc.vector.memset(wg_raw_scales[:].bitcast(I32), 0)
+        load_scale_rows(nc.scalar, wg_raw_scales, wg_scales)
         nc.gpsimd.memset(wd_plane[:].bitcast(I32), 0)
         nc.vector.memset(zero[:], 0.0)
+        nc.scalar.activation(no_bias[:], zero[:], ACT.Silu)
 
         nc.sync.dma_start(offsets[:], offs)
-        nc.sync.dma_start(out=wg_raw[:], in_=words(wg_words))
-        nc.sync.dma_start(out=wgt_sb[:, :HALF], in_=wgt[:, :HALF])
-        nc.sync.dma_start(out=planes[0][:], in_=x_planes[0])
-        load_scale_rows(nc.scalar, wg_raw_scales, wg_scales)
-        nc.scalar.activation(no_bias[:], zero[:], ACT.Silu)
-        nc.sync.dma_start(out=wgt_sb[:, HALF:], in_=wgt[:, HALF:])
-        for i in range(1, PACK):
-            nc.sync.dma_start(out=planes[i][:], in_=x_planes[i])
-        for h in range(2):
-            nc.sync.dma_start(out=wu_raw[h][:], in_=wu_rows[:, :, h * (R // 2) : (h + 1) * (R // 2)])
-        nc.sync.dma_start(out=wd_codes[:], in_=words(wd_words))
+        for what in LOADS:
+            if what == "wg":
+                nc.sync.dma_start(out=wg_raw[:], in_=words(wg_words))
+            elif what == "wgs":
+                pass
+            elif what == "wgt0":
+                nc.sync.dma_start(out=wgt_sb[:, :WGT_SPLIT], in_=wgt[:, :WGT_SPLIT])
+            elif what == "wgt1":
+                nc.sync.dma_start(out=wgt_sb[:, WGT_SPLIT:], in_=wgt[:, WGT_SPLIT:])
+            elif what[0] == "x":
+                nc.sync.dma_start(out=planes[int(what[1])][:], in_=x_planes[int(what[1])])
+            elif what == "wd":
+                nc.sync.dma_start(out=wd_codes[:], in_=words(wd_words))
+            elif what == "wu":
+                nc.sync.dma_start(out=wu_raw[:], in_=wu_rows)
+            elif what == "wgt":
+                nc.sync.dma_start(out=wgt_sb[:], in_=wgt)
+            else:
+                half = slice(int(what[2]) * (R // 2), (int(what[2]) + 1) * (R // 2))
+                nc.sync.dma_start(out=wu_raw[:, :, half], in_=wu_rows[:, :, half])
         load_scale_rows(nc.sync, wd_plane, wd_scales)
         with nc.allow_non_contiguous_dma(reason="one bias value a partition"):
             nc.sync.dma_start(out=bias[:], in_=b.rearrange("(u p) -> p u", p=P))
@@ -143,13 +168,12 @@ def tile_list_silu_bias_kernel(
             copy_on(
                 engine,
                 wu_bf[:, :, 64 * h : 64 * (h + 1), :].rearrange("p t m i -> p m i t"),
-                wu_raw[h][:].rearrange("p i (m t) -> p m i t", t=PACK),
+                wu_raw[:, :, h * (R // 2) : (h + 1) * (R // 2)].rearrange("p i (m t) -> p m i t", t=PACK),
             )
 
         def gate_chunk(c):
             first, last = c * CHUNK, (c + 1) * CHUNK
-            quantize(xg_codes, xg_plane, xg_bf, first, last)
-            ga = psum.tile([P, PACK, CHUNK], F32, name="ga", bufs=2)
+            ga = psum.tile([P, PACK, CHUNK], F32, name="ga", bufs=BUFS[0])
             for t in range(PACK):
                 product(ga[:, t, :], wg_codes, wg_plane, t, xg_codes, xg_plane, first, last)
             nc.scalar.activation(
@@ -158,7 +182,7 @@ def tile_list_silu_bias_kernel(
 
         def up_chunk(c):
             first, last = c * CHUNK, (c + 1) * CHUNK
-            ub = psum.tile([P, PACK, CHUNK], F32, name="ub", bufs=2)
+            ub = psum.tile([P, PACK, CHUNK], F32, name="ub", bufs=BUFS[1])
             for t in range(PACK):
                 product(ub[:, t, :], wu_codes, wu_plane, t, xg_codes, xg_plane, first, last)
             nc.vector.tensor_tensor(
@@ -167,7 +191,7 @@ def tile_list_silu_bias_kernel(
 
         def down(first, last, engines):
             for pair in range(2):
-                y = psum.tile([P, 2, last - first], F32, name="y", bufs=4)
+                y = psum.tile([P, 2, last - first], F32, name="y", bufs=BUFS[2])
                 for s in range(2):
                     product(y[:, s, :], wd_codes, wd_plane, 2 * pair + s, h_codes, h_plane, first, last)
                 for s in range(2):
@@ -178,44 +202,70 @@ def tile_list_silu_bias_kernel(
                         )
                     else:
                         nc.vector.tensor_scalar_add(result[:, u, first:last], y[:, s, :], bias[:, u : u + 1])
-                nc.sync.dma_start(
-                    out=out_rows[:, 2 * pair : 2 * pair + 2, first:last],
-                    in_=result[:, 2 * pair : 2 * pair + 2, first:last],
-                )
+                if last // CHUNK in STORES:
+                    begin = STORES[last // CHUNK] * CHUNK
+                    nc.sync.dma_start(
+                        out=out_rows[:, 2 * pair : 2 * pair + 2, begin:last],
+                        in_=result[:, 2 * pair : 2 * pair + 2, begin:last],
+                    )
 
-        for i in range(PACK - 1):
-            for first in (0, HALF):
-                gather(i, first, first + HALF)
-                if i == 1:
-                    round_pair("scalar", 0, first, first + HALF)
-
-        for step in range(CHUNKS + 2):
-            if step < CHUNKS:
-                gather(PACK - 1, step * CHUNK, (step + 1) * CHUNK)
-            if 1 <= step <= CHUNKS:
-                c = step - 1
-                round_pair("scalar" if c < 4 else "vector", 2, c * CHUNK, (c + 1) * CHUNK)
-            if step == 4:
-                round_wu("scalar", 0)
-            if step == 7:
-                round_wu("vector", 1)
-            if step == 8:
+        def wu_work(step):
+            for h in range(2):
+                if step == WU_STEPS[h]:
+                    round_wu(WU_ENGINES[h], h)
+            if step == WU_STEPS[2]:
                 nc.vector.quantize_mx(
                     out=wu_codes[:].bitcast(FP8X4),
                     scales=wu_plane[:],
                     in_=wu_bf[:].rearrange("p t m i -> p (t m i)"),
                 )
-            if step >= 2:
-                gate_chunk(step - 2)
 
-        spans = {1: (0, 256, ("scalar", "scalar")), 3: (256, 512, ("scalar", "scalar")),
-                 5: (512, 768, ("scalar", "scalar")), 6: (768, 896, ("scalar", "scalar")),
-                 7: (896, 1024, ("scalar", "vector"))}
-        for step in range(CHUNKS + 1):
-            if step < CHUNKS:
-                up_chunk(step)
-            if step >= 1:
-                c = step - 1
-                quantize(h_codes, h_plane, h_bf, c * CHUNK, (c + 1) * CHUNK)
-                if c in spans:
-                    down(*spans[c])
+        for i in range(PACK - 1):
+            first = 0
+            for width in EARLY:
+                gather(i, first, first + width)
+                if i == 1:
+                    round_pair("scalar", 0, first, first + width)
+                first += width
+            wu_work(i - PACK + 1)
+
+        begin = 0
+        for end in STORE_ENDS:
+            STORES[end] = begin
+            begin = end
+        picks, downs = {}, {}
+        c = 0
+        for width, engine in PICK_SPANS:
+            picks[c] = (c * CHUNK, (c + width) * CHUNK, engine)
+            c += width
+        c = 0
+        for width, one, other in DOWN_SPANS:
+            downs[c + width - 1] = (c * CHUNK, (c + width) * CHUNK, (one, other))
+            c += width
+
+        def stage(which, step):
+            if which == 0 and step in picks:
+                gather(PACK - 1, picks[step][0], picks[step][1])
+            if which == 1 and step - 1 in picks:
+                round_pair(picks[step - 1][2], 2, picks[step - 1][0], picks[step - 1][1])
+            if which == 2:
+                wu_work(step)
+            c = step - GATE_LAG
+            if which == 3:
+                if c in picks:
+                    quantize(xg_codes, xg_plane, xg_bf, picks[c][0], picks[c][1])
+                if 0 <= c < CHUNKS:
+                    gate_chunk(c)
+            c -= UP_LAG
+            if which == 4 and 0 <= c < CHUNKS:
+                up_chunk(c)
+            c -= 1
+            if which == 5 and c in downs:
+                quantize(h_codes, h_plane, h_bf, downs[c][0], downs[c][1])
+            c -= DOWN_LAG
+            if which == 6 and c in downs:
+                down(*downs[c])
+
+        for step in range(CHUNKS + GATE_LAG + UP_LAG + DOWN_LAG + 1):
+            for which in STAGE_ORDER:
+                stage(which, step)

@@ -16,24 +16,26 @@ ACT = mybir.ActivationFunctionType
 
 P = 128
 PACK = 4
+QUADRANTS, QUADRANT = 4, 32
+SCALE_ROWS = 4
+PICKS_PER_COLUMN = 16
+LINE_WORDS = 4
+MX_ALIGN = 64
+
 CHUNK = 128
 CHUNKS = J // CHUNK
-HALF = J // 2
-PER_COLUMN = 16
-LOADS = ["wgt0","x0","wgt1","x1","wg","wgs","x2","x3","wu0","wu1","wd"]
-PICK_SPANS = [[1,"vector"],[1,"vector"],[1,"scalar"],[1,"scalar"],[1,"vector"],[1,"scalar"],[1,"scalar"],[1,"scalar"]]
-WU_ENGINES = ["scalar","vector"]
-WU_STEPS = [-1,3,3]
-UP_LAG = 4
-DOWN_SPANS = [[2,"scalar","scalar"],[2,"scalar","scalar"],[1,"vector","scalar"],[1,"scalar","scalar"],[1,"scalar","vector"],[1,"vector","scalar"]]
-WGT_SPLIT = 512
-EARLY = (512, 512)
-BUFS = (2, 2, 4)
-STAGE_ORDER = (0, 1, 2, 3, 4, 5, 6)
-GATE_LAG = 2
-DOWN_LAG = 1
-STORE_ENDS = [2,4,5,6,7,8]
-STORES = {}
+SPAN_CHUNKS = 2
+SPAN = SPAN_CHUNKS * CHUNK
+HALF_J = J // 2
+HALF_R = R // 2
+
+GA_BANKS, UB_BANKS, Y_BANKS = 2, 3, 3
+
+VECTOR_ROUNDS = (0, 1, 4)
+VECTOR_BIASES = ((2, 1), (3, 0))
+
+ROUND_LAG, GATE_LAG, UP_LAG, QUANTIZE_H_LAG, DOWN_LAG = 1, 2, 8, 9, 10
+ROUND_WU_STEP, QUANTIZE_WU_STEP = 0, 4
 
 
 def tile_list_silu_bias_kernel(
@@ -44,228 +46,195 @@ def tile_list_silu_bias_kernel(
         keep = ctx.enter_context(tc.tile_pool(name="keep", bufs=1))
         psum = ctx.enter_context(tc.psum_pool(name="psum", bufs=1))
 
-        offsets = keep.tile([P, J // PER_COLUMN], U16, name="offsets")
+        offsets = keep.tile([P, J // PICKS_PER_COLUMN], U16, name="offsets")
         planes = [keep.tile([P, T], F32, name="plane%d" % i) for i in range(PACK)]
         wgt_sb = keep.tile([P, J], F32, name="wgt_sb")
-        wg_raw = keep.tile([P, R], I32, name="wg_raw", align_bytes=64)
-        wg_raw_scales = keep.tile([P, R], U8, name="wg_raw_scales", align_bytes=64)
-        wg_codes = keep.tile([P, R], I32, name="wg_codes", align_bytes=64)
-        wg_plane = keep.tile([P, R], U8, name="wg_plane", align_bytes=64)
-        wu_raw = keep.tile([P, PACK, R], F32, name="wu_raw")
-        wu_bf = keep.tile([P, PACK, P, PACK], BF16, name="wu_bf", align_bytes=64)
-        wu_codes = keep.tile([P, R], I32, name="wu_codes", align_bytes=64)
-        wu_plane = keep.tile([P, R], U8, name="wu_plane", align_bytes=64)
-        wd_codes = keep.tile([P, N], I32, name="wd_codes", align_bytes=64)
-        wd_plane = keep.tile([P, N], U8, name="wd_plane", align_bytes=64)
+        wg_loaded_words = keep.tile([P, R], I32, name="wg_loaded_words", align_bytes=MX_ALIGN)
+        wg_loaded_scales = keep.tile([P, R], U8, name="wg_loaded_scales", align_bytes=MX_ALIGN)
+        wg_mx_words = keep.tile([P, R], I32, name="wg_mx_words", align_bytes=MX_ALIGN)
+        wg_mx_scales = keep.tile([P, R], U8, name="wg_mx_scales", align_bytes=MX_ALIGN)
+        wu_loaded = keep.tile([P, PACK, R], F32, name="wu_loaded")
+        wu_bf = keep.tile([P, PACK, P, PACK], BF16, name="wu_bf", align_bytes=MX_ALIGN)
+        wu_mx_words = keep.tile([P, R], I32, name="wu_mx_words", align_bytes=MX_ALIGN)
+        wu_mx_scales = keep.tile([P, R], U8, name="wu_mx_scales", align_bytes=MX_ALIGN)
+        wd_mx_words = keep.tile([P, N], I32, name="wd_mx_words", align_bytes=MX_ALIGN)
+        wd_mx_scales = keep.tile([P, N], U8, name="wd_mx_scales", align_bytes=MX_ALIGN)
         bias = keep.tile([P, N // P], F32, name="bias")
         zero = keep.tile([P, 1], F32, name="zero")
-        no_bias = keep.tile([P, 1], F32, name="no_bias")
-        picked = keep.tile([P, PACK, J], F32, name="picked")
-        xg_bf = keep.tile([P, J, PACK], BF16, name="xg_bf", align_bytes=64)
-        xg_codes = keep.tile([P, J], I32, name="xg_codes", align_bytes=64)
-        xg_plane = keep.tile([P, J], U8, name="xg_plane", align_bytes=64)
+        silu_of_zero = keep.tile([P, 1], F32, name="silu_of_zero")
+        xg = keep.tile([P, PACK, J], F32, name="xg")
+        xg_bf = keep.tile([P, J, PACK], BF16, name="xg_bf", align_bytes=MX_ALIGN)
+        xg_mx_words = keep.tile([P, J], I32, name="xg_mx_words", align_bytes=MX_ALIGN)
+        xg_mx_scales = keep.tile([P, J], U8, name="xg_mx_scales", align_bytes=MX_ALIGN)
         gate = keep.tile([P, J, PACK], F32, name="gate")
-        h_bf = keep.tile([P, J, PACK], BF16, name="h_bf", align_bytes=64)
-        h_codes = keep.tile([P, J], I32, name="h_codes", align_bytes=64)
-        h_plane = keep.tile([P, J], U8, name="h_plane", align_bytes=64)
+        h_bf = keep.tile([P, J, PACK], BF16, name="h_bf", align_bytes=MX_ALIGN)
+        h_mx_words = keep.tile([P, J], I32, name="h_mx_words", align_bytes=MX_ALIGN)
+        h_mx_scales = keep.tile([P, J], U8, name="h_mx_scales", align_bytes=MX_ALIGN)
         result = keep.tile([P, N // P, J], F32, name="result")
+
+        wg_mx, wu_mx, wd_mx = (wg_mx_words, wg_mx_scales), (wu_mx_words, wu_mx_scales), (wd_mx_words, wd_mx_scales)
+        xg_mx, h_mx = (xg_mx_words, xg_mx_scales), (h_mx_words, h_mx_scales)
 
         x_planes = xT.rearrange("(p i) t -> i p t", i=PACK)
         wu_rows = wu.rearrange("(p i) r -> p i r", i=PACK)
-        out_rows = out.rearrange("(u p) j -> p u j", p=P)
+        out_tiles = out.rearrange("(u p) j -> p u j", p=P)
 
-        def words(dram):
-            return dram[0].rearrange("p n i -> p (n i)").bitcast(I32)
+        def load_words(tile, dram):
+            nc.sync.dma_start(out=tile[:], in_=dram[0].rearrange("p n i -> p (n i)").bitcast(I32))
 
-        def load_scale_rows(queue, plane, dram):
-            for q in range(4):
-                queue.dma_start(
-                    out=plane[32 * q : 32 * q + 4, :].bitcast(I32),
-                    in_=dram[0, 4 * q : 4 * q + 4, :].bitcast(I32),
+        def load_scale_rows(tile, dram):
+            for q in range(QUADRANTS):
+                nc.sync.dma_start(
+                    out=tile[QUADRANT * q : QUADRANT * q + SCALE_ROWS, :].bitcast(I32),
+                    in_=dram[0, SCALE_ROWS * q : SCALE_ROWS * (q + 1), :].bitcast(I32),
                 )
 
-        nc.vector.memset(wg_raw_scales[:].bitcast(I32), 0)
-        load_scale_rows(nc.scalar, wg_raw_scales, wg_scales)
-        nc.gpsimd.memset(wd_plane[:].bitcast(I32), 0)
+        def load_plane(i):
+            nc.sync.dma_start(out=planes[i][:], in_=x_planes[i])
+
+        nc.gpsimd.memset(wg_loaded_scales[:].bitcast(I32), 0)
+        nc.gpsimd.memset(wd_mx_scales[:].bitcast(I32), 0)
         nc.vector.memset(zero[:], 0.0)
-        nc.scalar.activation(no_bias[:], zero[:], ACT.Silu)
+        nc.scalar.activation(silu_of_zero[:], zero[:], ACT.Silu)
 
         nc.sync.dma_start(offsets[:], offs)
-        for what in LOADS:
-            if what == "wg":
-                nc.sync.dma_start(out=wg_raw[:], in_=words(wg_words))
-            elif what == "wgs":
-                pass
-            elif what == "wgt0":
-                nc.sync.dma_start(out=wgt_sb[:, :WGT_SPLIT], in_=wgt[:, :WGT_SPLIT])
-            elif what == "wgt1":
-                nc.sync.dma_start(out=wgt_sb[:, WGT_SPLIT:], in_=wgt[:, WGT_SPLIT:])
-            elif what[0] == "x":
-                nc.sync.dma_start(out=planes[int(what[1])][:], in_=x_planes[int(what[1])])
-            elif what == "wd":
-                nc.sync.dma_start(out=wd_codes[:], in_=words(wd_words))
-            elif what == "wu":
-                nc.sync.dma_start(out=wu_raw[:], in_=wu_rows)
-            elif what == "wgt":
-                nc.sync.dma_start(out=wgt_sb[:], in_=wgt)
-            else:
-                half = slice(int(what[2]) * (R // 2), (int(what[2]) + 1) * (R // 2))
-                nc.sync.dma_start(out=wu_raw[:, :, half], in_=wu_rows[:, :, half])
-        load_scale_rows(nc.sync, wd_plane, wd_scales)
+        nc.sync.dma_start(out=wgt_sb[:, :HALF_J], in_=wgt[:, :HALF_J])
+        load_plane(0)
+        nc.sync.dma_start(out=wgt_sb[:, HALF_J:], in_=wgt[:, HALF_J:])
+        load_scale_rows(wg_loaded_scales, wg_scales)
+        load_plane(1)
+        load_words(wg_loaded_words, wg_words)
+        load_plane(2)
+        load_plane(3)
+        for first in (0, HALF_R):
+            nc.sync.dma_start(out=wu_loaded[:, :, first : first + HALF_R], in_=wu_rows[:, :, first : first + HALF_R])
+        load_words(wd_mx_words, wd_words)
+        load_scale_rows(wd_mx_scales, wd_scales)
         with nc.allow_non_contiguous_dma(reason="one bias value a partition"):
             nc.sync.dma_start(out=bias[:], in_=b.rearrange("(u p) -> p u", p=P))
 
         nc.vector.tensor_copy(
-            out=wg_codes[:].rearrange("p (t m) -> p m t", t=PACK),
-            in_=wg_raw[:].rearrange("p (m t) -> p m t", t=PACK),
+            out=wg_mx_words[:].rearrange("p (t a m) -> p a t m", t=PACK, m=LINE_WORDS),
+            in_=wg_loaded_words[:].rearrange("p (a m t) -> p a t m", t=PACK, m=LINE_WORDS),
         )
         nc.vector.tensor_copy(
-            out=wg_plane[:].rearrange("p (t m) -> p m t", t=PACK),
-            in_=wg_raw_scales[:].rearrange("p (m t) -> p m t", t=PACK),
+            out=wg_mx_scales[:].rearrange("p (t m) -> p t m", t=PACK),
+            in_=wg_loaded_scales[:].rearrange("p (m t) -> p t m", t=PACK),
         )
 
         def gather(i, first, last):
-            nc.vector.tensor_tensor(
-                picked[:, i, first:last],
-                planes[i][:].indirect(offsets[:, first // PER_COLUMN : last // PER_COLUMN]),
-                wgt_sb[:, first:last],
-                MULT,
-            )
+            picks = offsets[:, first // PICKS_PER_COLUMN : last // PICKS_PER_COLUMN]
+            nc.vector.tensor_tensor(xg[:, i, first:last], planes[i][:].indirect(picks), wgt_sb[:, first:last], MULT)
 
-        def copy_on(engine, dst, src):
-            if engine == "scalar":
-                nc.scalar.copy(out=dst, in_=src)
-            else:
+        def round_to_bf16(on_vector, dst, src):
+            if on_vector:
                 nc.vector.tensor_copy(out=dst, in_=src)
+            else:
+                nc.scalar.copy(out=dst, in_=src)
 
-        def round_pair(engine, i, first, last):
-            copy_on(
-                engine,
-                xg_bf[:, first:last, i : i + 2],
-                picked[:, i : i + 2, first:last].rearrange("p i j -> p j i"),
+        def round_plane_pair(on_vector, i, first, last):
+            round_to_bf16(
+                on_vector, xg_bf[:, first:last, i : i + 2], xg[:, i : i + 2, first:last].rearrange("p i j -> p j i")
             )
 
-        def quantize(codes, plane, src, first, last):
+        def round_wu_half(on_vector, half):
+            per_tile = HALF_R // PACK
+            round_to_bf16(
+                on_vector,
+                wu_bf[:, :, half * per_tile : (half + 1) * per_tile, :].rearrange("p t m i -> p m t i"),
+                wu_loaded[:, :, half * HALF_R : (half + 1) * HALF_R].rearrange("p i (m t) -> p m t i", t=PACK),
+            )
+
+        def quantize(operand, src, first, last):
+            words, scales = operand
             nc.vector.quantize_mx(
-                out=codes[:, first:last].bitcast(FP8X4),
-                scales=plane[:, first:last],
-                in_=src[:, first:last, :].rearrange("p j i -> p (j i)"),
+                out=words[:, first:last].bitcast(FP8X4),
+                scales=scales[:, first:last],
+                in_=src[:, first:last, :].rearrange("p c i -> p (c i)"),
             )
 
-        def product(dst, w_codes, w_plane, tile, a_codes, a_plane, first, last):
-            cols = slice(tile * P, (tile + 1) * P)
+        def product(dst, weight, column_tile, moving, first, last):
+            cols = slice(column_tile * P, (column_tile + 1) * P)
             nc.tensor.matmul_mx(
                 out=dst,
-                lhsT=w_codes[:, cols].bitcast(FP8X4),
-                lhsT_scale=w_plane[:, cols],
-                rhs=a_codes[:, first:last].bitcast(FP8X4),
-                rhs_scale=a_plane[:, first:last],
+                lhsT=weight[0][:, cols].bitcast(FP8X4),
+                lhsT_scale=weight[1][:, cols],
+                rhs=moving[0][:, first:last].bitcast(FP8X4),
+                rhs_scale=moving[1][:, first:last],
                 start=True,
                 stop=True,
             )
 
-        def round_wu(engine, h):
-            copy_on(
-                engine,
-                wu_bf[:, :, 64 * h : 64 * (h + 1), :].rearrange("p t m i -> p m i t"),
-                wu_raw[:, :, h * (R // 2) : (h + 1) * (R // 2)].rearrange("p i (m t) -> p m i t", t=PACK),
-            )
-
         def gate_chunk(c):
             first, last = c * CHUNK, (c + 1) * CHUNK
-            ga = psum.tile([P, PACK, CHUNK], F32, name="ga", bufs=BUFS[0])
+            quantize(xg_mx, xg_bf, first, last)
+            ga = psum.tile([P, PACK, CHUNK], F32, name="ga", bufs=GA_BANKS)
             for t in range(PACK):
-                product(ga[:, t, :], wg_codes, wg_plane, t, xg_codes, xg_plane, first, last)
+                product(ga[:, t, :], wg_mx, t, xg_mx, first, last)
             nc.scalar.activation(
-                gate[:, first:last, :], ga[:].rearrange("p t j -> p j t"), ACT.Silu, bias=no_bias[:]
+                gate[:, first:last, :], ga[:].rearrange("p t j -> p j t"), ACT.Silu, bias=silu_of_zero[:]
             )
 
         def up_chunk(c):
             first, last = c * CHUNK, (c + 1) * CHUNK
-            ub = psum.tile([P, PACK, CHUNK], F32, name="ub", bufs=BUFS[1])
+            ub = psum.tile([P, PACK, CHUNK], F32, name="ub", bufs=UB_BANKS)
             for t in range(PACK):
-                product(ub[:, t, :], wu_codes, wu_plane, t, xg_codes, xg_plane, first, last)
+                product(ub[:, t, :], wu_mx, t, xg_mx, first, last)
             nc.vector.tensor_tensor(
                 h_bf[:, first:last, :], ub[:].rearrange("p t j -> p j t"), gate[:, first:last, :], MULT
             )
 
-        def down(first, last, engines):
+        def store(first_tile, last_tile, first, last):
+            nc.sync.dma_start(
+                out=out_tiles[:, first_tile:last_tile, first:last], in_=result[:, first_tile:last_tile, first:last]
+            )
+
+        def down_span(span):
+            first, last = span * SPAN, (span + 1) * SPAN
             for pair in range(2):
-                y = psum.tile([P, 2, last - first], F32, name="y", bufs=BUFS[2])
+                y = psum.tile([P, 2, SPAN], F32, name="y", bufs=Y_BANKS)
                 for s in range(2):
-                    product(y[:, s, :], wd_codes, wd_plane, 2 * pair + s, h_codes, h_plane, first, last)
+                    product(y[:, s, :], wd_mx, 2 * pair + s, h_mx, first, last)
                 for s in range(2):
                     u = 2 * pair + s
-                    if engines[pair] == "scalar":
+                    if (span, pair) in VECTOR_BIASES:
+                        nc.vector.tensor_scalar_add(result[:, u, first:last], y[:, s, :], bias[:, u : u + 1])
+                    else:
                         nc.scalar.activation(
                             result[:, u, first:last], y[:, s, :], ACT.Identity, bias=bias[:, u : u + 1]
                         )
-                    else:
-                        nc.vector.tensor_scalar_add(result[:, u, first:last], y[:, s, :], bias[:, u : u + 1])
-                if last // CHUNK in STORES:
-                    begin = STORES[last // CHUNK] * CHUNK
-                    nc.sync.dma_start(
-                        out=out_rows[:, 2 * pair : 2 * pair + 2, begin:last],
-                        in_=result[:, 2 * pair : 2 * pair + 2, begin:last],
-                    )
+                    if last == J:
+                        store(u, u + 1, first, last)
+                if last < J:
+                    store(2 * pair, 2 * pair + 2, first, last)
 
-        def wu_work(step):
-            for h in range(2):
-                if step == WU_STEPS[h]:
-                    round_wu(WU_ENGINES[h], h)
-            if step == WU_STEPS[2]:
-                nc.vector.quantize_mx(
-                    out=wu_codes[:].bitcast(FP8X4),
-                    scales=wu_plane[:],
-                    in_=wu_bf[:].rearrange("p t m i -> p (t m i)"),
-                )
+        def span_ending_at(c):
+            return c // SPAN_CHUNKS if 0 <= c < CHUNKS and c % SPAN_CHUNKS == SPAN_CHUNKS - 1 else None
 
         for i in range(PACK - 1):
-            first = 0
-            for width in EARLY:
-                gather(i, first, first + width)
+            for first in (0, HALF_J):
+                gather(i, first, first + HALF_J)
                 if i == 1:
-                    round_pair("scalar", 0, first, first + width)
-                first += width
-            wu_work(i - PACK + 1)
+                    round_plane_pair(False, 0, first, first + HALF_J)
 
-        begin = 0
-        for end in STORE_ENDS:
-            STORES[end] = begin
-            begin = end
-        picks, downs = {}, {}
-        c = 0
-        for width, engine in PICK_SPANS:
-            picks[c] = (c * CHUNK, (c + width) * CHUNK, engine)
-            c += width
-        c = 0
-        for width, one, other in DOWN_SPANS:
-            downs[c + width - 1] = (c * CHUNK, (c + width) * CHUNK, (one, other))
-            c += width
-
-        def stage(which, step):
-            if which == 0 and step in picks:
-                gather(PACK - 1, picks[step][0], picks[step][1])
-            if which == 1 and step - 1 in picks:
-                round_pair(picks[step - 1][2], 2, picks[step - 1][0], picks[step - 1][1])
-            if which == 2:
-                wu_work(step)
-            c = step - GATE_LAG
-            if which == 3:
-                if c in picks:
-                    quantize(xg_codes, xg_plane, xg_bf, picks[c][0], picks[c][1])
-                if 0 <= c < CHUNKS:
-                    gate_chunk(c)
-            c -= UP_LAG
-            if which == 4 and 0 <= c < CHUNKS:
-                up_chunk(c)
-            c -= 1
-            if which == 5 and c in downs:
-                quantize(h_codes, h_plane, h_bf, downs[c][0], downs[c][1])
-            c -= DOWN_LAG
-            if which == 6 and c in downs:
-                down(*downs[c])
-
-        for step in range(CHUNKS + GATE_LAG + UP_LAG + DOWN_LAG + 1):
-            for which in STAGE_ORDER:
-                stage(which, step)
+        for step in range(CHUNKS + DOWN_LAG):
+            c = step - ROUND_LAG
+            if 0 <= c < CHUNKS:
+                round_plane_pair(c in VECTOR_ROUNDS, 2, c * CHUNK, (c + 1) * CHUNK)
+            span = span_ending_at(step - QUANTIZE_H_LAG)
+            if span is not None:
+                quantize(h_mx, h_bf, span * SPAN, (span + 1) * SPAN)
+            if 0 <= step - GATE_LAG < CHUNKS:
+                gate_chunk(step - GATE_LAG)
+            if step == ROUND_WU_STEP:
+                round_wu_half(False, 0)
+                round_wu_half(True, 1)
+            if step == QUANTIZE_WU_STEP:
+                quantize(wu_mx, wu_bf[:].rearrange("p t m i -> p (t m) i"), 0, R)
+            if 0 <= step - UP_LAG < CHUNKS:
+                up_chunk(step - UP_LAG)
+            if step < CHUNKS:
+                gather(PACK - 1, step * CHUNK, (step + 1) * CHUNK)
+            span = span_ending_at(step - DOWN_LAG)
+            if span is not None:
+                down_span(span)

from contextlib import ExitStack

import concourse.mybir as mybir

K, R, N, T, J = 512, 512, 512, 2048, 1024
FLOPS = 2 * J * (2 * K * R + R * N)

F32 = mybir.dt.float32
BF16 = mybir.dt.bfloat16
I32 = mybir.dt.int32
U16 = mybir.dt.uint16
U8 = mybir.dt.uint8
FP8X4 = mybir.dt.float8_e4m3fn_x4
MULT = mybir.AluOpType.mult
ACT = mybir.ActivationFunctionType

P = 128
PACK = 4
QUADRANTS, QUADRANT = 4, 32
SCALE_ROWS = 4
PICKS_PER_COLUMN = 16
LINE_WORDS = 4
MX_ALIGN = 64

CHUNK = 128
CHUNKS = J // CHUNK
SPAN_CHUNKS = 2
SPAN = SPAN_CHUNKS * CHUNK
HALF_J = J // 2
HALF_R = R // 2

GA_BANKS, UB_BANKS, Y_BANKS = 2, 3, 3

VECTOR_ROUNDS = (0, 1, 4)
VECTOR_BIASES = ((2, 1), (3, 0))

ROUND_LAG, GATE_LAG, UP_LAG, QUANTIZE_H_LAG, DOWN_LAG = 1, 2, 8, 9, 10
ROUND_WU_STEP, QUANTIZE_WU_STEP = 0, 4


def tile_list_silu_bias_kernel(
    tc, xT, wgt, wg_words, wg_scales, wu, wd_words, wd_scales, b, offs, out
):
    nc = tc.nc
    with ExitStack() as ctx:
        keep = ctx.enter_context(tc.tile_pool(name="keep", bufs=1))
        psum = ctx.enter_context(tc.psum_pool(name="psum", bufs=1))

        offsets = keep.tile([P, J // PICKS_PER_COLUMN], U16, name="offsets")
        planes = [keep.tile([P, T], F32, name="plane%d" % i) for i in range(PACK)]
        wgt_sb = keep.tile([P, J], F32, name="wgt_sb")
        wg_loaded_words = keep.tile([P, R], I32, name="wg_loaded_words", align_bytes=MX_ALIGN)
        wg_loaded_scales = keep.tile([P, R], U8, name="wg_loaded_scales", align_bytes=MX_ALIGN)
        wg_mx_words = keep.tile([P, R], I32, name="wg_mx_words", align_bytes=MX_ALIGN)
        wg_mx_scales = keep.tile([P, R], U8, name="wg_mx_scales", align_bytes=MX_ALIGN)
        wu_loaded = keep.tile([P, PACK, R], F32, name="wu_loaded")
        wu_bf = keep.tile([P, PACK, P, PACK], BF16, name="wu_bf", align_bytes=MX_ALIGN)
        wu_mx_words = keep.tile([P, R], I32, name="wu_mx_words", align_bytes=MX_ALIGN)
        wu_mx_scales = keep.tile([P, R], U8, name="wu_mx_scales", align_bytes=MX_ALIGN)
        wd_mx_words = keep.tile([P, N], I32, name="wd_mx_words", align_bytes=MX_ALIGN)
        wd_mx_scales = keep.tile([P, N], U8, name="wd_mx_scales", align_bytes=MX_ALIGN)
        bias = keep.tile([P, N // P], F32, name="bias")
        zero = keep.tile([P, 1], F32, name="zero")
        silu_of_zero = keep.tile([P, 1], F32, name="silu_of_zero")
        xg = keep.tile([P, PACK, J], F32, name="xg")
        xg_bf = keep.tile([P, J, PACK], BF16, name="xg_bf", align_bytes=MX_ALIGN)
        xg_mx_words = keep.tile([P, J], I32, name="xg_mx_words", align_bytes=MX_ALIGN)
        xg_mx_scales = keep.tile([P, J], U8, name="xg_mx_scales", align_bytes=MX_ALIGN)
        gate = keep.tile([P, J, PACK], F32, name="gate")
        h_bf = keep.tile([P, J, PACK], BF16, name="h_bf", align_bytes=MX_ALIGN)
        h_mx_words = keep.tile([P, J], I32, name="h_mx_words", align_bytes=MX_ALIGN)
        h_mx_scales = keep.tile([P, J], U8, name="h_mx_scales", align_bytes=MX_ALIGN)
        result = keep.tile([P, N // P, J], F32, name="result")

        wg_mx, wu_mx, wd_mx = (wg_mx_words, wg_mx_scales), (wu_mx_words, wu_mx_scales), (wd_mx_words, wd_mx_scales)
        xg_mx, h_mx = (xg_mx_words, xg_mx_scales), (h_mx_words, h_mx_scales)

        x_planes = xT.rearrange("(p i) t -> i p t", i=PACK)
        wu_rows = wu.rearrange("(p i) r -> p i r", i=PACK)
        out_tiles = out.rearrange("(u p) j -> p u j", p=P)

        def load_words(tile, dram):
            nc.sync.dma_start(out=tile[:], in_=dram[0].rearrange("p n i -> p (n i)").bitcast(I32))

        def load_scale_rows(tile, dram):
            for q in range(QUADRANTS):
                nc.sync.dma_start(
                    out=tile[QUADRANT * q : QUADRANT * q + SCALE_ROWS, :].bitcast(I32),
                    in_=dram[0, SCALE_ROWS * q : SCALE_ROWS * (q + 1), :].bitcast(I32),
                )

        def load_plane(i):
            nc.sync.dma_start(out=planes[i][:], in_=x_planes[i])

        nc.gpsimd.memset(wg_loaded_scales[:].bitcast(I32), 0)
        nc.gpsimd.memset(wd_mx_scales[:].bitcast(I32), 0)
        nc.vector.memset(zero[:], 0.0)
        nc.scalar.activation(silu_of_zero[:], zero[:], ACT.Silu)

        nc.sync.dma_start(offsets[:], offs)
        nc.sync.dma_start(out=wgt_sb[:, :HALF_J], in_=wgt[:, :HALF_J])
        load_plane(0)
        nc.sync.dma_start(out=wgt_sb[:, HALF_J:], in_=wgt[:, HALF_J:])
        load_scale_rows(wg_loaded_scales, wg_scales)
        load_plane(1)
        load_words(wg_loaded_words, wg_words)
        load_plane(2)
        load_plane(3)
        for first in (0, HALF_R):
            nc.sync.dma_start(out=wu_loaded[:, :, first : first + HALF_R], in_=wu_rows[:, :, first : first + HALF_R])
        load_words(wd_mx_words, wd_words)
        load_scale_rows(wd_mx_scales, wd_scales)
        with nc.allow_non_contiguous_dma(reason="one bias value a partition"):
            nc.sync.dma_start(out=bias[:], in_=b.rearrange("(u p) -> p u", p=P))

        nc.vector.tensor_copy(
            out=wg_mx_words[:].rearrange("p (t a m) -> p a t m", t=PACK, m=LINE_WORDS),
            in_=wg_loaded_words[:].rearrange("p (a m t) -> p a t m", t=PACK, m=LINE_WORDS),
        )
        nc.vector.tensor_copy(
            out=wg_mx_scales[:].rearrange("p (t m) -> p t m", t=PACK),
            in_=wg_loaded_scales[:].rearrange("p (m t) -> p t m", t=PACK),
        )

        def gather(i, first, last):
            picks = offsets[:, first // PICKS_PER_COLUMN : last // PICKS_PER_COLUMN]
            nc.vector.tensor_tensor(xg[:, i, first:last], planes[i][:].indirect(picks), wgt_sb[:, first:last], MULT)

        def round_to_bf16(on_vector, dst, src):
            if on_vector:
                nc.vector.tensor_copy(out=dst, in_=src)
            else:
                nc.scalar.copy(out=dst, in_=src)

        def round_plane_pair(on_vector, i, first, last):
            round_to_bf16(
                on_vector, xg_bf[:, first:last, i : i + 2], xg[:, i : i + 2, first:last].rearrange("p i j -> p j i")
            )

        def round_wu_half(on_vector, half):
            per_tile = HALF_R // PACK
            round_to_bf16(
                on_vector,
                wu_bf[:, :, half * per_tile : (half + 1) * per_tile, :].rearrange("p t m i -> p m t i"),
                wu_loaded[:, :, half * HALF_R : (half + 1) * HALF_R].rearrange("p i (m t) -> p m t i", t=PACK),
            )

        def quantize(operand, src, first, last):
            words, scales = operand
            nc.vector.quantize_mx(
                out=words[:, first:last].bitcast(FP8X4),
                scales=scales[:, first:last],
                in_=src[:, first:last, :].rearrange("p c i -> p (c i)"),
            )

        def product(dst, weight, column_tile, moving, first, last):
            cols = slice(column_tile * P, (column_tile + 1) * P)
            nc.tensor.matmul_mx(
                out=dst,
                lhsT=weight[0][:, cols].bitcast(FP8X4),
                lhsT_scale=weight[1][:, cols],
                rhs=moving[0][:, first:last].bitcast(FP8X4),
                rhs_scale=moving[1][:, first:last],
                start=True,
                stop=True,
            )

        def gate_chunk(c):
            first, last = c * CHUNK, (c + 1) * CHUNK
            quantize(xg_mx, xg_bf, first, last)
            ga = psum.tile([P, PACK, CHUNK], F32, name="ga", bufs=GA_BANKS)
            for t in range(PACK):
                product(ga[:, t, :], wg_mx, t, xg_mx, first, last)
            nc.scalar.activation(
                gate[:, first:last, :], ga[:].rearrange("p t j -> p j t"), ACT.Silu, bias=silu_of_zero[:]
            )

        def up_chunk(c):
            first, last = c * CHUNK, (c + 1) * CHUNK
            ub = psum.tile([P, PACK, CHUNK], F32, name="ub", bufs=UB_BANKS)
            for t in range(PACK):
                product(ub[:, t, :], wu_mx, t, xg_mx, first, last)
            nc.vector.tensor_tensor(
                h_bf[:, first:last, :], ub[:].rearrange("p t j -> p j t"), gate[:, first:last, :], MULT
            )

        def store(first_tile, last_tile, first, last):
            nc.sync.dma_start(
                out=out_tiles[:, first_tile:last_tile, first:last], in_=result[:, first_tile:last_tile, first:last]
            )

        def down_span(span):
            first, last = span * SPAN, (span + 1) * SPAN
            for pair in range(2):
                y = psum.tile([P, 2, SPAN], F32, name="y", bufs=Y_BANKS)
                for s in range(2):
                    product(y[:, s, :], wd_mx, 2 * pair + s, h_mx, first, last)
                for s in range(2):
                    u = 2 * pair + s
                    if (span, pair) in VECTOR_BIASES:
                        nc.vector.tensor_scalar_add(result[:, u, first:last], y[:, s, :], bias[:, u : u + 1])
                    else:
                        nc.scalar.activation(
                            result[:, u, first:last], y[:, s, :], ACT.Identity, bias=bias[:, u : u + 1]
                        )
                    if last == J:
                        store(u, u + 1, first, last)
                if last < J:
                    store(2 * pair, 2 * pair + 2, first, last)

        def span_ending_at(c):
            return c // SPAN_CHUNKS if 0 <= c < CHUNKS and c % SPAN_CHUNKS == SPAN_CHUNKS - 1 else None

        for i in range(PACK - 1):
            for first in (0, HALF_J):
                gather(i, first, first + HALF_J)
                if i == 1:
                    round_plane_pair(False, 0, first, first + HALF_J)

        for step in range(CHUNKS + DOWN_LAG):
            c = step - ROUND_LAG
            if 0 <= c < CHUNKS:
                round_plane_pair(c in VECTOR_ROUNDS, 2, c * CHUNK, (c + 1) * CHUNK)
            span = span_ending_at(step - QUANTIZE_H_LAG)
            if span is not None:
                quantize(h_mx, h_bf, span * SPAN, (span + 1) * SPAN)
            if 0 <= step - GATE_LAG < CHUNKS:
                gate_chunk(step - GATE_LAG)
            if step == ROUND_WU_STEP:
                round_wu_half(False, 0)
                round_wu_half(True, 1)
            if step == QUANTIZE_WU_STEP:
                quantize(wu_mx, wu_bf[:].rearrange("p t m i -> p (t m) i"), 0, R)
            if 0 <= step - UP_LAG < CHUNKS:
                up_chunk(step - UP_LAG)
            if step < CHUNKS:
                gather(PACK - 1, step * CHUNK, (step + 1) * CHUNK)
            span = span_ending_at(step - DOWN_LAG)
            if span is not None:
                down_span(span)
